import numpy as np
import ml_dtypes


def mxq(x, axis, fmt="e4m3"):
    dtype, down = {"e4m3": (ml_dtypes.float8_e4m3fn, 7), "e5m2": (ml_dtypes.float8_e5m2, 14)}[fmt]
    v = np.moveaxis(np.asarray(x, np.float32).astype(ml_dtypes.bfloat16).astype(np.float64), axis, -1)
    blocks = v.reshape(v.shape[:-1] + (-1, 32))
    amax = np.abs(blocks).max(-1, keepdims=True)
    byte = np.maximum(np.where(amax > 0, np.frexp(amax)[1] - 1 + 127, 0) - down, 1)
    scale = np.exp2(byte - 127.0)
    codes = (blocks / scale).astype(np.float32).astype(dtype).astype(np.float64)
    return np.moveaxis((codes * scale).reshape(v.shape), -1, axis)


WIDE = False


def mx_kscale(k):
    if not WIDE:
        return np.ones(k)
    levels = np.array([10, -10, 5, -5, 0])
    if k % 512:
        return np.exp2(np.random.permutation(np.resize(levels, k // 32))).repeat(32)
    a = np.empty((k // 512, 16))
    for p in range(k // 512):
        a[p, :8] = np.random.permutation(np.resize(levels, 8))
        for g in range(8):
            far = levels[np.abs(levels - a[p, g]) >= 10]
            a[p, g + 8] = far[np.random.randint(len(far))]
    return np.exp2(a.ravel()).repeat(32)


def f64(x):
    return np.asarray(x).astype(np.float64)


def striped8(idx):
    return np.asarray(idx).reshape(8, -1, 16).transpose(0, 2, 1).reshape(128, -1).astype(np.uint16)


def unstriped8(offs):
    return offs.reshape(8, 16, -1).transpose(0, 2, 1).reshape(8, -1).astype(np.int64)


def pick8(x, idx, run):
    r = np.arange(len(x))
    return x[r[:, None], idx[r % (8 * run) // run]]


E2M1 = np.array([0.0, 0.5, 1.0, 1.5, 2.0, 3.0, 4.0, 6.0, -0.0, -0.5, -1.0, -1.5, -2.0, -3.0, -4.0, -6.0])


def pack_weight(w, fmt):
    k, n = w.shape
    w = f64(np.asarray(w, np.float32).astype(ml_dtypes.bfloat16)).reshape(k // 32, 32, n)
    amax = np.abs(w).max(1)
    if fmt == "e4m3":
        byte = np.frexp(amax)[1] - 1 + 127 - 7
    else:
        mant, ex = np.frexp(amax / 6.0)
        byte = np.where(mant > 0.5, ex, ex - 1) + 127
    byte = np.clip(np.where(amax > 0, byte, 1), 1, 254)
    scaled = (w * np.exp2(127.0 - byte)[:, None, :]).reshape(k, n).astype(np.float32)
    by_word = np.ascontiguousarray(scaled.reshape(k // 512, 128, 4, n).transpose(0, 1, 3, 2))
    if fmt == "e4m3":
        words = by_word.astype(ml_dtypes.float8_e4m3fn).view(np.uint8)
    else:
        c = by_word.astype(ml_dtypes.float4_e2m1fn).view(np.uint8) & 0xF
        words = (c[..., 0::2] | (c[..., 1::2] << 4)).reshape(k // 512, 128, 2 * n)
    return np.ascontiguousarray(words), np.ascontiguousarray(byte.astype(np.uint8).reshape(k // 512, 16, n))


def unpack_weight(words, scales, fmt):
    g, _, n = scales.shape
    words = np.ascontiguousarray(words).reshape(g, 128, n, -1)
    if fmt == "e4m3":
        vals = words.view(ml_dtypes.float8_e4m3fn).astype(np.float64)
    else:
        nib = np.empty((g, 128, n, 4), np.uint8)
        nib[..., 0::2] = words & 0xF
        nib[..., 1::2] = words >> 4
        vals = E2M1[nib]
    vals = vals * np.repeat(np.exp2(scales.astype(np.float64) - 127.0), 8, axis=1)[..., None]
    return vals.transpose(0, 1, 3, 2).reshape(g * 512, n)


D, T, U, X, I, Q = 512, 1024, 1024, 1024, 512, 128


def setup_inputs():
    n = np.random.standard_normal
    idx = np.stack([np.random.permutation(T)[:I] for _ in range(8)])
    idx2 = np.stack([np.random.permutation(U)[:I] for _ in range(8)])
    idx3 = np.stack([np.random.permutation(X)[:I] for _ in range(8)])
    idx4 = np.stack([np.random.permutation(X)[:I] for _ in range(8)])
    fd = mx_kscale(D)
    cachep = pack_weight(n((D, T)) / fd[:, None], "e2m1")
    draftp = pack_weight(n((D, U)) / fd[:, None], "e4m3")
    archp = pack_weight(n((D, X)) / fd[:, None], "e2m1")
    return {
        "query": (n((D, Q)) * 1.0 / np.sqrt(D) * fd[:, None]).astype(np.float32),
        "cache_words": cachep[0],
        "cache_scales": cachep[1],
        "draft_words": draftp[0],
        "draft_scales": draftp[1],
        "arch_words": archp[0],
        "arch_scales": archp[1],
        "offs": striped8(idx),
        "offs2": striped8(idx2),
        "offs3": striped8(idx3),
        "offs4": striped8(idx4),
    }


def reference(query, cache_words, cache_scales, draft_words, draft_scales, arch_words, arch_scales, offs, offs2, offs3, offs4):
    idx = unstriped8(offs)
    idx2 = unstriped8(offs2)
    idx3 = unstriped8(offs3)
    idx4 = unstriped8(offs4)
    cacheu = unpack_weight(cache_words, cache_scales, "e2m1")
    draftu = unpack_weight(draft_words, draft_scales, "e4m3")
    archu = unpack_weight(arch_words, arch_scales, "e2m1")
    queryq = mxq(f64(query), 0, "e4m3")
    a = queryq.T @ cacheu
    b = queryq.T @ draftu
    c0 = queryq.T @ archu
    w = np.abs(pick8(a, idx, 16) - pick8(b, idx2, 16))
    v = np.abs(pick8(b, idx2, 16) - pick8(c0, idx3, 16))
    r = w - v
    f1 = np.zeros((Q, X))
    f1[np.arange(Q)[:, None], idx4[np.arange(Q) % 128 // 16]] = r
    cc = c0 + f1
    y = np.abs(pick8(cc, idx3, 16) - w)
    return y

@@ -1,0 +1,157 @@
+from contextlib import ExitStack
+
+import concourse.mybir as mybir
+
+F32 = mybir.dt.float32
+BF16 = mybir.dt.bfloat16
+I32 = mybir.dt.int32
+U32 = mybir.dt.uint32
+U16 = mybir.dt.uint16
+U8 = mybir.dt.uint8
+FP8X4 = mybir.dt.float8_e4m3fn_x4
+FP4X4 = mybir.dt.float4_e2m1fn_x4
+ALU = mybir.AluOpType
+ACT = mybir.ActivationFunctionType
+
+P = 128
+PACK = 4
+TOKENS = 1024
+SLOTS = 512
+BANK = 512
+HALF = SLOTS // 2
+LIST_COLS = HALF // 16
+FLOPS = 3 * 2 * 512 * 128 * 1024
+
+
+def tile_attend_gapenergies_three_kernel(
+    tc, query, cache_words, cache_scales, draft_words, draft_scales, arch_words, arch_scales, offs, offs2, offs3, offs4, out
+):
+    nc = tc.nc
+    with ExitStack() as ctx:
+        sb = ctx.enter_context(tc.tile_pool(name="sb", bufs=1))
+        ps = ctx.enter_context(tc.psum_pool(name="ps", bufs=1))
+
+        def plane_tile(name, base):
+            tile = sb.tile([P, 2 * TOKENS], U8, name=name, align_bytes=64)
+            nc.vector.memset(tile[base : base + 64, :].bitcast(I32), 0)
+            return tile
+
+        def load_plane(tile, scales, base, first_row):
+            rows = scales[0].bitcast(I32).rearrange("(h q j) c -> q j h c", h=2, q=2)
+            for q in range(2):
+                p0 = base + 32 * q + first_row
+                nc.sync.dma_start(
+                    out=tile[p0 : p0 + 4, :].bitcast(I32).rearrange("p (h c) -> p h c", h=2), in_=rows[q]
+                )
+
+        def spread_plane(tile, base):
+            live = base // 64
+            words = tile[:].bitcast(I32)
+            quarter = TOKENS // 4
+            nc.vector.tensor_copy(
+                out=words[64 - base : 128 - base, live * quarter : (live + 1) * quarter],
+                in_=words[base : base + 64, (1 - live) * quarter : (2 - live) * quarter],
+            )
+
+        draft_plane = plane_tile("draft_plane", 0)
+        cache_plane = plane_tile("cache_plane", 0)
+        arch_plane = plane_tile("arch_plane", 64)
+        f1 = sb.tile([P, TOKENS], F32, name="f1")
+        nc.vector.memset(f1[:], 0.0)
+
+        q_raw = sb.tile([P, PACK, P], F32, name="q_raw")
+        nc.sync.dma_start(out=q_raw[:], in_=query.rearrange("(p j) q -> p j q", j=PACK))
+        load_plane(draft_plane, draft_scales, 0, 4)
+        draft_rows = draft_words[0].rearrange("p n t -> p (n t)").bitcast(I32)
+        draft_codes = []
+        for n in range(2):
+            tile = sb.tile([P, BANK], I32, name="draft_codes%d" % n, align_bytes=64)
+            nc.sync.dma_start(out=tile[:], in_=draft_rows[:, n * BANK : (n + 1) * BANK])
+            draft_codes.append(tile)
+        load_plane(cache_plane, cache_scales, 0, 0)
+        cache_codes = sb.tile([P, 2 * TOKENS], U8, name="cache_codes", align_bytes=64)
+        nc.sync.dma_start(out=cache_codes[:].bitcast(I32), in_=cache_words[0].bitcast(I32))
+        arch_codes = sb.tile([P, 2 * TOKENS], U8, name="arch_codes", align_bytes=64)
+        nc.sync.dma_start(out=arch_codes[:].bitcast(I32), in_=arch_words[0].bitcast(I32))
+        load_plane(arch_plane, arch_scales, 64, 0)
+        lists = {}
+        for name, src in (("draft", offs2), ("cache", offs), ("arch", offs3), ("put", offs4)):
+            lists[name] = sb.tile([P, SLOTS // 16], U16, name="list_" + name)
+            nc.sync.dma_start(lists[name][:], src)
+
+        def half_list(name, h):
+            return lists[name][:, h * LIST_COLS : (h + 1) * LIST_COLS]
+
+        q_bf = sb.tile([P, P, PACK], BF16, name="q_bf", align_bytes=64)
+        nc.vector.tensor_copy(out=q_bf[:], in_=q_raw[:].rearrange("p j q -> p q j"))
+        spread_plane(draft_plane, 0)
+        q_codes = sb.tile([P, P], U32, name="q_codes", align_bytes=64)
+        q_plane = sb.tile([P, P], U8, name="q_plane", align_bytes=64)
+        nc.vector.quantize_mx(out=q_codes[:].bitcast(FP8X4), scales=q_plane[:], in_=q_bf[:].rearrange("p q j -> p (q j)"))
+        spread_plane(cache_plane, 0)
+        spread_plane(arch_plane, 64)
+
+        def score(name, n, rhs, rhs_scale):
+            bank = ps.tile([P, BANK], F32, name="bank_%s%d" % (name, n))
+            nc.tensor.matmul_mx(
+                out=bank[:], lhsT=q_codes[:].bitcast(FP8X4), lhsT_scale=q_plane[:], rhs=rhs, rhs_scale=rhs_scale, start=True, stop=True
+            )
+            return bank
+
+        b_banks = [score("b", n, draft_codes[n][:].bitcast(FP8X4), draft_plane[4:P, n * BANK : (n + 1) * BANK]) for n in range(2)]
+        a_banks = [
+            score("a", n, cache_codes[:, 2 * n * BANK : 2 * (n + 1) * BANK].bitcast(FP4X4), cache_plane[:, n * BANK : (n + 1) * BANK])
+            for n in range(2)
+        ]
+        c_banks = [
+            score(
+                "c",
+                n,
+                arch_codes[:, 2 * n * BANK : 2 * (n + 1) * BANK].bitcast(FP4X4),
+                arch_plane[:, TOKENS + n * BANK : TOKENS + (n + 1) * BANK],
+            )
+            for n in range(2)
+        ]
+
+        a = sb.tile([P, TOKENS], F32, name="a")
+        b = sb.tile([P, TOKENS], F32, name="b")
+        c0 = sb.tile([P, TOKENS], F32, name="c0")
+        gb = [sb.tile([P, HALF], F32, name="gb%d" % h) for h in range(2)]
+        dw = [sb.tile([P, HALF], F32, name="dw%d" % h) for h in range(2)]
+        dv = [sb.tile([P, HALF], F32, name="dv%d" % h) for h in range(2)]
+        w = [sb.tile([P, HALF], F32, name="w%d" % h) for h in range(2)]
+        v = [sb.tile([P, HALF], F32, name="v%d" % h) for h in range(2)]
+        r = [sb.tile([P, HALF], F32, name="r%d" % h) for h in range(2)]
+
+        nc.scalar.copy(b[:, :BANK], b_banks[0][:])
+        nc.vector.tensor_copy(b[:, BANK:], b_banks[1][:])
+        nc.scalar.copy(a[:, :BANK], a_banks[0][:])
+        nc.vector.tensor_copy(gb[0][:], b[:].indirect(half_list("draft", 0)))
+        nc.vector.tensor_copy(a[:, BANK:], a_banks[1][:])
+        nc.scalar.copy(c0[:, :BANK], c_banks[0][:])
+        nc.scalar.copy(c0[:, BANK:], c_banks[1][:])
+        nc.vector.tensor_tensor(dw[0][:], a[:].indirect(half_list("cache", 0)), gb[0][:], ALU.subtract)
+        nc.scalar.activation(w[0][:], dw[0][:], ACT.Abs)
+        nc.vector.tensor_tensor(dv[0][:], c0[:].indirect(half_list("arch", 0)), gb[0][:], ALU.subtract)
+        nc.scalar.activation(gb[1][:], b[:].indirect(half_list("draft", 1)), ACT.Copy)
+        nc.scalar.activation(v[0][:], dv[0][:], ACT.Abs)
+        nc.vector.tensor_tensor(dw[1][:], a[:].indirect(half_list("cache", 1)), gb[1][:], ALU.subtract)
+        nc.vector.tensor_tensor(r[0][:], w[0][:], v[0][:], ALU.subtract)
+        nc.scalar.activation(f1[:].indirect(half_list("put", 0)), r[0][:], ACT.Copy)
+        nc.vector.tensor_tensor(dv[1][:], c0[:].indirect(half_list("arch", 1)), gb[1][:], ALU.subtract)
+        nc.vector.scalar_tensor_tensor(w[1][:], dw[1][:], -1.0, dw[1][:], ALU.mult, ALU.max)
+        nc.vector.scalar_tensor_tensor(v[1][:], dv[1][:], -1.0, dv[1][:], ALU.mult, ALU.max)
+        nc.vector.tensor_tensor(r[1][:], w[1][:], v[1][:], ALU.subtract)
+        nc.scalar.activation(f1[:].indirect(half_list("put", 1)), r[1][:], ACT.Copy)
+
+        cc = sb.tile([P, TOKENS], F32, name="cc")
+        nc.vector.tensor_tensor(cc[:], c0[:], f1[:], ALU.add)
+        dy = [sb.tile([P, HALF], F32, name="dy%d" % h) for h in range(2)]
+        y = [sb.tile([P, HALF], F32, name="y%d" % h) for h in range(2)]
+        gcc = sb.tile([P, HALF], F32, name="gcc")
+        nc.vector.tensor_tensor(dy[0][:], cc[:].indirect(half_list("arch", 0)), w[0][:], ALU.subtract)
+        nc.scalar.activation(gcc[:], cc[:].indirect(half_list("arch", 1)), ACT.Copy)
+        nc.vector.tensor_tensor(dy[1][:], gcc[:], w[1][:], ALU.subtract)
+        for h in range(2):
+            nc.scalar.activation(y[h][:], dy[h][:], ACT.Abs)
+            nc.sync.dma_start(out=out[:, h * HALF : (h + 1) * HALF], in_=y[h][:])

@@ -19,6 +19,7 @@ TOKENS = 1024
 SLOTS = 512
 BANK = 512
 HALF = SLOTS // 2
+QUARTER = SLOTS // 4
 LIST_COLS = HALF // 16
 FLOPS = 3 * 2 * 512 * 128 * 1024
 
@@ -31,65 +32,69 @@ def tile_attend_gapenergies_three_kernel(
         sb = ctx.enter_context(tc.tile_pool(name="sb", bufs=1))
         ps = ctx.enter_context(tc.psum_pool(name="ps", bufs=1))
 
-        def plane_tile(name, base):
+        plane_words = TOKENS // 4
+
+        def plane_tile(name):
             tile = sb.tile([P, 2 * TOKENS], U8, name=name, align_bytes=64)
-            nc.vector.memset(tile[base : base + 64, :].bitcast(I32), 0)
+            nc.vector.memset(tile[:, :TOKENS].bitcast(I32), 0)
             return tile
 
-        def load_plane(tile, scales, base, first_row):
-            rows = scales[0].bitcast(I32).rearrange("(h q j) c -> q j h c", h=2, q=2)
-            for q in range(2):
-                p0 = base + 32 * q + first_row
-                nc.sync.dma_start(
-                    out=tile[p0 : p0 + 4, :].bitcast(I32).rearrange("p (h c) -> p h c", h=2), in_=rows[q]
+        def load_plane(queue, tile, scales):
+            rows = scales[0].bitcast(I32).rearrange("(h q j) c -> h j q c", h=2, q=2)
+            for h in range(2):
+                queue.dma_start(out=tile[64 * h : 64 * h + 4, :].bitcast(I32).rearrange("p (q c) -> p q c", q=2), in_=rows[h])
+
+        def spread_plane(tile):
+            words = tile[:].bitcast(I32)
+            for h in range(2):
+                nc.vector.tensor_copy(
+                    out=words[64 * h + 32 : 64 * h + 36, :plane_words], in_=words[64 * h : 64 * h + 4, plane_words:]
                 )
 
-        def spread_plane(tile, base):
-            live = base // 64
-            words = tile[:].bitcast(I32)
-            quarter = TOKENS // 4
-            nc.vector.tensor_copy(
-                out=words[64 - base : 128 - base, live * quarter : (live + 1) * quarter],
-                in_=words[base : base + 64, (1 - live) * quarter : (2 - live) * quarter],
-            )
-
-        draft_plane = plane_tile("draft_plane", 0)
-        cache_plane = plane_tile("cache_plane", 0)
-        arch_plane = plane_tile("arch_plane", 64)
-        f1 = sb.tile([P, TOKENS], F32, name="f1")
-        nc.vector.memset(f1[:], 0.0)
+        draft_plane = plane_tile("draft_plane")
+        f1 = [sb.tile([P, TOKENS], F32, name="f1_%d" % k) for k in range(2)]
+        nc.vector.memset(f1[0][:], 0.0)
+        cache_plane = plane_tile("cache_plane")
+        arch_plane = plane_tile("arch_plane")
 
         q_raw = sb.tile([P, PACK, P], F32, name="q_raw")
         nc.sync.dma_start(out=q_raw[:], in_=query.rearrange("(p j) q -> p j q", j=PACK))
-        load_plane(draft_plane, draft_scales, 0, 4)
+        load_plane(nc.sync, draft_plane, draft_scales)
+        load_plane(nc.scalar, cache_plane, cache_scales)
         draft_rows = draft_words[0].rearrange("p n t -> p (n t)").bitcast(I32)
         draft_codes = []
         for n in range(2):
             tile = sb.tile([P, BANK], I32, name="draft_codes%d" % n, align_bytes=64)
             nc.sync.dma_start(out=tile[:], in_=draft_rows[:, n * BANK : (n + 1) * BANK])
             draft_codes.append(tile)
-        load_plane(cache_plane, cache_scales, 0, 0)
+        load_plane(nc.scalar, arch_plane, arch_scales)
         cache_codes = sb.tile([P, 2 * TOKENS], U8, name="cache_codes", align_bytes=64)
         nc.sync.dma_start(out=cache_codes[:].bitcast(I32), in_=cache_words[0].bitcast(I32))
-        arch_codes = sb.tile([P, 2 * TOKENS], U8, name="arch_codes", align_bytes=64)
-        nc.sync.dma_start(out=arch_codes[:].bitcast(I32), in_=arch_words[0].bitcast(I32))
-        load_plane(arch_plane, arch_scales, 64, 0)
         lists = {}
-        for name, src in (("draft", offs2), ("cache", offs), ("arch", offs3), ("put", offs4)):
+
+        def load_list(name, src):
             lists[name] = sb.tile([P, SLOTS // 16], U16, name="list_" + name)
             nc.sync.dma_start(lists[name][:], src)
+
+        load_list("draft", offs2)
+        arch_codes = sb.tile([P, 2 * TOKENS], U8, name="arch_codes", tag="arch_then_gb1", align_bytes=64)
+        nc.sync.dma_start(out=arch_codes[:].bitcast(I32), in_=arch_words[0].bitcast(I32))
+        load_list("arch", offs3)
+        load_list("cache", offs)
+        load_list("put", offs4)
 
         def half_list(name, h):
             return lists[name][:, h * LIST_COLS : (h + 1) * LIST_COLS]
 
         q_bf = sb.tile([P, P, PACK], BF16, name="q_bf", align_bytes=64)
         nc.vector.tensor_copy(out=q_bf[:], in_=q_raw[:].rearrange("p j q -> p q j"))
-        spread_plane(draft_plane, 0)
+        spread_plane(draft_plane)
         q_codes = sb.tile([P, P], U32, name="q_codes", align_bytes=64)
         q_plane = sb.tile([P, P], U8, name="q_plane", align_bytes=64)
         nc.vector.quantize_mx(out=q_codes[:].bitcast(FP8X4), scales=q_plane[:], in_=q_bf[:].rearrange("p q j -> p (q j)"))
-        spread_plane(cache_plane, 0)
-        spread_plane(arch_plane, 64)
+        spread_plane(cache_plane)
+        spread_plane(arch_plane)
+        nc.gpsimd.memset(f1[1][:], 0.0)
 
         def score(name, n, rhs, rhs_scale):
             bank = ps.tile([P, BANK], F32, name="bank_%s%d" % (name, n))
@@ -98,7 +103,7 @@ def tile_attend_gapenergies_three_kernel(
             )
             return bank
 
-        b_banks = [score("b", n, draft_codes[n][:].bitcast(FP8X4), draft_plane[4:P, n * BANK : (n + 1) * BANK]) for n in range(2)]
+        b_banks = [score("b", n, draft_codes[n][:].bitcast(FP8X4), draft_plane[:, n * BANK : (n + 1) * BANK]) for n in range(2)]
         a_banks = [
             score("a", n, cache_codes[:, 2 * n * BANK : 2 * (n + 1) * BANK].bitcast(FP4X4), cache_plane[:, n * BANK : (n + 1) * BANK])
             for n in range(2)
@@ -108,7 +113,7 @@ def tile_attend_gapenergies_three_kernel(
                 "c",
                 n,
                 arch_codes[:, 2 * n * BANK : 2 * (n + 1) * BANK].bitcast(FP4X4),
-                arch_plane[:, TOKENS + n * BANK : TOKENS + (n + 1) * BANK],
+                arch_plane[:, n * BANK : (n + 1) * BANK],
             )
             for n in range(2)
         ]
@@ -116,42 +121,53 @@ def tile_attend_gapenergies_three_kernel(
         a = sb.tile([P, TOKENS], F32, name="a")
         b = sb.tile([P, TOKENS], F32, name="b")
         c0 = sb.tile([P, TOKENS], F32, name="c0")
-        gb = [sb.tile([P, HALF], F32, name="gb%d" % h) for h in range(2)]
-        dw = [sb.tile([P, HALF], F32, name="dw%d" % h) for h in range(2)]
-        dv = [sb.tile([P, HALF], F32, name="dv%d" % h) for h in range(2)]
-        w = [sb.tile([P, HALF], F32, name="w%d" % h) for h in range(2)]
-        v = [sb.tile([P, HALF], F32, name="v%d" % h) for h in range(2)]
-        r = [sb.tile([P, HALF], F32, name="r%d" % h) for h in range(2)]
+        gb0 = sb.tile([P, HALF], F32, name="gb0")
+        dw0 = sb.tile([P, HALF], F32, name="dw0")
+        dv0 = sb.tile([P, HALF], F32, name="dv0")
+        w0 = sb.tile([P, HALF], F32, name="w0")
+        gc1 = sb.tile([P, HALF], F32, name="gc1")
+        d1 = sb.tile([P, SLOTS], F32, name="d1")
+        wide = sb.tile([P, HALF + TOKENS], F32, name="wide")
+        wv1 = wide[:, :SLOTS]
+        r0 = [sb.tile([P, QUARTER], F32, name="r0_%d" % k) for k in range(2)]
+        r1 = sb.tile([P, HALF], F32, name="r1")
+        w = [w0[:], wv1[:, :HALF]]
 
-        nc.scalar.copy(b[:, :BANK], b_banks[0][:])
-        nc.vector.tensor_copy(b[:, BANK:], b_banks[1][:])
-        nc.scalar.copy(a[:, :BANK], a_banks[0][:])
-        nc.vector.tensor_copy(gb[0][:], b[:].indirect(half_list("draft", 0)))
-        nc.vector.tensor_copy(a[:, BANK:], a_banks[1][:])
-        nc.scalar.copy(c0[:, :BANK], c_banks[0][:])
+        for whole, banks in ((b, b_banks), (a, a_banks)):
+            for n in range(2):
+                nc.scalar.copy(whole[:, n * BANK : (n + 1) * BANK], banks[n][:])
+        nc.vector.tensor_copy(gb0[:], b[:].indirect(half_list("draft", 0)))
+        nc.vector.tensor_copy(c0[:, :BANK], c_banks[0][:])
         nc.scalar.copy(c0[:, BANK:], c_banks[1][:])
-        nc.vector.tensor_tensor(dw[0][:], a[:].indirect(half_list("cache", 0)), gb[0][:], ALU.subtract)
-        nc.scalar.activation(w[0][:], dw[0][:], ACT.Abs)
-        nc.vector.tensor_tensor(dv[0][:], c0[:].indirect(half_list("arch", 0)), gb[0][:], ALU.subtract)
-        nc.scalar.activation(gb[1][:], b[:].indirect(half_list("draft", 1)), ACT.Copy)
-        nc.scalar.activation(v[0][:], dv[0][:], ACT.Abs)
-        nc.vector.tensor_tensor(dw[1][:], a[:].indirect(half_list("cache", 1)), gb[1][:], ALU.subtract)
-        nc.vector.tensor_tensor(r[0][:], w[0][:], v[0][:], ALU.subtract)
-        nc.scalar.activation(f1[:].indirect(half_list("put", 0)), r[0][:], ACT.Copy)
-        nc.vector.tensor_tensor(dv[1][:], c0[:].indirect(half_list("arch", 1)), gb[1][:], ALU.subtract)
-        nc.vector.scalar_tensor_tensor(w[1][:], dw[1][:], -1.0, dw[1][:], ALU.mult, ALU.max)
-        nc.vector.scalar_tensor_tensor(v[1][:], dv[1][:], -1.0, dv[1][:], ALU.mult, ALU.max)
-        nc.vector.tensor_tensor(r[1][:], w[1][:], v[1][:], ALU.subtract)
-        nc.scalar.activation(f1[:].indirect(half_list("put", 1)), r[1][:], ACT.Copy)
+        nc.vector.tensor_tensor(dw0[:], a[:].indirect(half_list("cache", 0)), gb0[:], ALU.subtract)
+        nc.vector.tensor_tensor(dv0[:], c0[:].indirect(half_list("arch", 0)), gb0[:], ALU.subtract)
+        gb1 = sb.tile([P, HALF], F32, name="gb1", tag="arch_then_gb1", align_bytes=64)
+        nc.scalar.activation(gb1[:], b[:].indirect(half_list("draft", 1)), ACT.Copy)
+        nc.scalar.activation(gc1[:], c0[:].indirect(half_list("arch", 1)), ACT.Copy)
+        nc.scalar.activation(w0[:], dw0[:], ACT.Abs)
+        for k in range(2):
+            nc.scalar.activation(wv1[:, HALF + k * QUARTER : HALF + (k + 1) * QUARTER], dv0[:, k * QUARTER : (k + 1) * QUARTER], ACT.Abs)
+        nc.vector.tensor_tensor(d1[:, :HALF], a[:].indirect(half_list("cache", 1)), gb1[:], ALU.subtract)
+        nc.vector.tensor_tensor(d1[:, HALF:], gc1[:], gb1[:], ALU.subtract)
+        for k in range(2):
+            nc.vector.tensor_tensor(
+                r0[k][:], w0[:, k * QUARTER : (k + 1) * QUARTER], wv1[:, HALF + k * QUARTER : HALF + (k + 1) * QUARTER], ALU.subtract
+            )
+            nc.scalar.activation(f1[k][:].indirect(lists["put"][:, k * LIST_COLS // 2 : (k + 1) * LIST_COLS // 2]), r0[k][:], ACT.Copy)
+        nc.vector.scalar_tensor_tensor(wv1, d1[:], -1.0, d1[:], ALU.mult, ALU.max)
+        nc.vector.tensor_tensor(r1[:], wv1[:, :HALF], wv1[:, HALF:], ALU.subtract)
+        nc.scalar.activation(f1[0][:].indirect(half_list("put", 1)), r1[:], ACT.Copy)
 
         cc = sb.tile([P, TOKENS], F32, name="cc")
-        nc.vector.tensor_tensor(cc[:], c0[:], f1[:], ALU.add)
+        part = wide[:, HALF:]
+        nc.vector.tensor_tensor(part, c0[:], f1[1][:], ALU.add)
+        nc.vector.tensor_tensor(cc[:], part, f1[0][:], ALU.add)
         dy = [sb.tile([P, HALF], F32, name="dy%d" % h) for h in range(2)]
         y = [sb.tile([P, HALF], F32, name="y%d" % h) for h in range(2)]
         gcc = sb.tile([P, HALF], F32, name="gcc")
-        nc.vector.tensor_tensor(dy[0][:], cc[:].indirect(half_list("arch", 0)), w[0][:], ALU.subtract)
+        nc.vector.tensor_tensor(dy[0][:], cc[:].indirect(half_list("arch", 0)), w[0], ALU.subtract)
         nc.scalar.activation(gcc[:], cc[:].indirect(half_list("arch", 1)), ACT.Copy)
-        nc.vector.tensor_tensor(dy[1][:], gcc[:], w[1][:], ALU.subtract)
+        nc.vector.tensor_tensor(dy[1][:], gcc[:], w[1], ALU.subtract)
         for h in range(2):
             nc.scalar.activation(y[h][:], dy[h][:], ACT.Abs)
             nc.sync.dma_start(out=out[:, h * HALF : (h + 1) * HALF], in_=y[h][:])

@@ -20,6 +20,7 @@ SLOTS = 512
 BANK = 512
 HALF = SLOTS // 2
 QUARTER = SLOTS // 4
+FIRST = 64
 LIST_COLS = HALF // 16
 FLOPS = 3 * 2 * 512 * 128 * 1024
 
@@ -34,9 +35,9 @@ def tile_attend_gapenergies_three_kernel(
 
         plane_words = TOKENS // 4
 
-        def plane_tile(name):
+        def plane_tile(engine, name):
             tile = sb.tile([P, 2 * TOKENS], U8, name=name, align_bytes=64)
-            nc.vector.memset(tile[:, :TOKENS].bitcast(I32), 0)
+            engine.memset(tile[:, :TOKENS].bitcast(I32), 0)
             return tile
 
         def load_plane(queue, tile, scales):
@@ -51,25 +52,26 @@ def tile_attend_gapenergies_three_kernel(
                     out=words[64 * h + 32 : 64 * h + 36, :plane_words], in_=words[64 * h : 64 * h + 4, plane_words:]
                 )
 
-        draft_plane = plane_tile("draft_plane")
+        draft_plane = plane_tile(nc.vector, "draft_plane")
+        cache_plane = plane_tile(nc.gpsimd, "cache_plane")
+        arch_plane = plane_tile(nc.vector, "arch_plane")
         f1 = [sb.tile([P, TOKENS], F32, name="f1_%d" % k) for k in range(2)]
         nc.vector.memset(f1[0][:], 0.0)
-        cache_plane = plane_tile("cache_plane")
-        arch_plane = plane_tile("arch_plane")
+        nc.gpsimd.memset(f1[1][:], 0.0)
 
         q_raw = sb.tile([P, PACK, P], F32, name="q_raw")
         nc.sync.dma_start(out=q_raw[:], in_=query.rearrange("(p j) q -> p j q", j=PACK))
-        load_plane(nc.sync, draft_plane, draft_scales)
-        load_plane(nc.scalar, cache_plane, cache_scales)
+        load_plane(nc.scalar, draft_plane, draft_scales)
+        load_plane(nc.sync, cache_plane, cache_scales)
         draft_rows = draft_words[0].rearrange("p n t -> p (n t)").bitcast(I32)
         draft_codes = []
         for n in range(2):
             tile = sb.tile([P, BANK], I32, name="draft_codes%d" % n, align_bytes=64)
             nc.sync.dma_start(out=tile[:], in_=draft_rows[:, n * BANK : (n + 1) * BANK])
             draft_codes.append(tile)
-        load_plane(nc.scalar, arch_plane, arch_scales)
         cache_codes = sb.tile([P, 2 * TOKENS], U8, name="cache_codes", align_bytes=64)
         nc.sync.dma_start(out=cache_codes[:].bitcast(I32), in_=cache_words[0].bitcast(I32))
+        load_plane(nc.sync, arch_plane, arch_scales)
         lists = {}
 
         def load_list(name, src):
@@ -94,7 +96,6 @@ def tile_attend_gapenergies_three_kernel(
         nc.vector.quantize_mx(out=q_codes[:].bitcast(FP8X4), scales=q_plane[:], in_=q_bf[:].rearrange("p q j -> p (q j)"))
         spread_plane(cache_plane)
         spread_plane(arch_plane)
-        nc.gpsimd.memset(f1[1][:], 0.0)
 
         def score(name, n, rhs, rhs_scale):
             bank = ps.tile([P, BANK], F32, name="bank_%s%d" % (name, n))
@@ -129,7 +130,10 @@ def tile_attend_gapenergies_three_kernel(
         d1 = sb.tile([P, SLOTS], F32, name="d1")
         wide = sb.tile([P, HALF + TOKENS], F32, name="wide")
         wv1 = wide[:, :SLOTS]
-        r0 = [sb.tile([P, QUARTER], F32, name="r0_%d" % k) for k in range(2)]
+        pieces = (slice(0, FIRST), slice(FIRST, HALF))
+        r0 = [sb.tile([P, piece.stop - piece.start], F32, name="r0_%d" % k) for k, piece in enumerate(pieces)]
+        v0_rest = sb.tile([P, HALF - FIRST], F32, name="v0_rest")
+        v0 = [wv1[:, HALF : HALF + FIRST], v0_rest[:]]
         r1 = sb.tile([P, HALF], F32, name="r1")
         w = [w0[:], wv1[:, :HALF]]
 
@@ -145,15 +149,13 @@ def tile_attend_gapenergies_three_kernel(
         nc.scalar.activation(gb1[:], b[:].indirect(half_list("draft", 1)), ACT.Copy)
         nc.scalar.activation(gc1[:], c0[:].indirect(half_list("arch", 1)), ACT.Copy)
         nc.scalar.activation(w0[:], dw0[:], ACT.Abs)
-        for k in range(2):
-            nc.scalar.activation(wv1[:, HALF + k * QUARTER : HALF + (k + 1) * QUARTER], dv0[:, k * QUARTER : (k + 1) * QUARTER], ACT.Abs)
+        for k, piece in enumerate(pieces):
+            nc.scalar.activation(v0[k], dv0[:, piece], ACT.Abs)
         nc.vector.tensor_tensor(d1[:, :HALF], a[:].indirect(half_list("cache", 1)), gb1[:], ALU.subtract)
         nc.vector.tensor_tensor(d1[:, HALF:], gc1[:], gb1[:], ALU.subtract)
-        for k in range(2):
-            nc.vector.tensor_tensor(
-                r0[k][:], w0[:, k * QUARTER : (k + 1) * QUARTER], wv1[:, HALF + k * QUARTER : HALF + (k + 1) * QUARTER], ALU.subtract
-            )
-            nc.scalar.activation(f1[k][:].indirect(lists["put"][:, k * LIST_COLS // 2 : (k + 1) * LIST_COLS // 2]), r0[k][:], ACT.Copy)
+        for k, piece in enumerate(pieces):
+            nc.vector.tensor_tensor(r0[k][:], w0[:, piece], v0[k], ALU.subtract)
+            nc.scalar.activation(f1[k][:].indirect(lists["put"][:, piece.start // 16 : piece.stop // 16]), r0[k][:], ACT.Copy)
         nc.vector.scalar_tensor_tensor(wv1, d1[:], -1.0, d1[:], ALU.mult, ALU.max)
         nc.vector.tensor_tensor(r1[:], wv1[:, :HALF], wv1[:, HALF:], ALU.subtract)
         nc.scalar.activation(f1[0][:].indirect(half_list("put", 1)), r1[:], ACT.Copy)
@@ -162,12 +164,17 @@ def tile_attend_gapenergies_three_kernel(
         part = wide[:, HALF:]
         nc.vector.tensor_tensor(part, c0[:], f1[1][:], ALU.add)
         nc.vector.tensor_tensor(cc[:], part, f1[0][:], ALU.add)
-        dy = [sb.tile([P, HALF], F32, name="dy%d" % h) for h in range(2)]
-        y = [sb.tile([P, HALF], F32, name="y%d" % h) for h in range(2)]
+        dy0 = sb.tile([P, HALF], F32, name="dy0")
+        y0 = sb.tile([P, HALF], F32, name="y0")
         gcc = sb.tile([P, HALF], F32, name="gcc")
-        nc.vector.tensor_tensor(dy[0][:], cc[:].indirect(half_list("arch", 0)), w[0], ALU.subtract)
+        nc.vector.tensor_tensor(dy0[:], cc[:].indirect(half_list("arch", 0)), w[0], ALU.subtract)
         nc.scalar.activation(gcc[:], cc[:].indirect(half_list("arch", 1)), ACT.Copy)
-        nc.vector.tensor_tensor(dy[1][:], gcc[:], w[1], ALU.subtract)
-        for h in range(2):
-            nc.scalar.activation(y[h][:], dy[h][:], ACT.Abs)
-            nc.sync.dma_start(out=out[:, h * HALF : (h + 1) * HALF], in_=y[h][:])
+        nc.scalar.activation(y0[:], dy0[:], ACT.Abs)
+        nc.sync.dma_start(out=out[:, :HALF], in_=y0[:])
+        for k in range(2):
+            cols = slice(k * QUARTER, (k + 1) * QUARTER)
+            dy1 = sb.tile([P, QUARTER], F32, name="dy1_%d" % k)
+            y1 = sb.tile([P, QUARTER], F32, name="y1_%d" % k)
+            nc.vector.tensor_tensor(dy1[:], gcc[:, cols], wv1[:, cols], ALU.subtract)
+            nc.scalar.activation(y1[:], dy1[:], ACT.Abs)
+            nc.sync.dma_start(out=out[:, HALF + cols.start : HALF + cols.stop], in_=y1[:])

@@ -53,22 +53,22 @@ def tile_attend_gapenergies_three_kernel(
                 )
 
         draft_plane = plane_tile(nc.vector, "draft_plane")
-        cache_plane = plane_tile(nc.gpsimd, "cache_plane")
+        cache_plane = plane_tile(nc.vector, "cache_plane")
         arch_plane = plane_tile(nc.vector, "arch_plane")
         f1 = [sb.tile([P, TOKENS], F32, name="f1_%d" % k) for k in range(2)]
         nc.vector.memset(f1[0][:], 0.0)
-        nc.gpsimd.memset(f1[1][:], 0.0)
+        nc.vector.memset(f1[1][:], 0.0)
 
         q_raw = sb.tile([P, PACK, P], F32, name="q_raw")
         nc.sync.dma_start(out=q_raw[:], in_=query.rearrange("(p j) q -> p j q", j=PACK))
-        load_plane(nc.scalar, draft_plane, draft_scales)
-        load_plane(nc.sync, cache_plane, cache_scales)
+        load_plane(nc.sync, draft_plane, draft_scales)
         draft_rows = draft_words[0].rearrange("p n t -> p (n t)").bitcast(I32)
         draft_codes = []
         for n in range(2):
             tile = sb.tile([P, BANK], I32, name="draft_codes%d" % n, align_bytes=64)
             nc.sync.dma_start(out=tile[:], in_=draft_rows[:, n * BANK : (n + 1) * BANK])
             draft_codes.append(tile)
+        load_plane(nc.sync, cache_plane, cache_scales)
         cache_codes = sb.tile([P, 2 * TOKENS], U8, name="cache_codes", align_bytes=64)
         nc.sync.dma_start(out=cache_codes[:].bitcast(I32), in_=cache_words[0].bitcast(I32))
         load_plane(nc.sync, arch_plane, arch_scales)

@@ -18,11 +18,12 @@ PACK = 4
 TOKENS = 1024
 SLOTS = 512
 BANK = 512
+PER_COLUMN = 16
 HALF = SLOTS // 2
-QUARTER = SLOTS // 4
+STORE = SLOTS // 4
+DRAFT_PASS = TOKENS // 4
 FIRST = 64
-LIST_COLS = HALF // 16
-FLOPS = 3 * 2 * 512 * 128 * 1024
+FLOPS = 3 * 2 * 512 * P * TOKENS
 
 
 def tile_attend_gapenergies_three_kernel(
@@ -33,92 +34,93 @@ def tile_attend_gapenergies_three_kernel(
         sb = ctx.enter_context(tc.tile_pool(name="sb", bufs=1))
         ps = ctx.enter_context(tc.psum_pool(name="ps", bufs=1))
 
-        plane_words = TOKENS // 4
-
-        def plane_tile(engine, name):
+        def fp4_plane(name):
             tile = sb.tile([P, 2 * TOKENS], U8, name=name, align_bytes=64)
-            engine.memset(tile[:, :TOKENS].bitcast(I32), 0)
+            nc.vector.memset(tile[:, :TOKENS].bitcast(I32), 0)
             return tile
 
-        def load_plane(queue, tile, scales):
-            rows = scales[0].bitcast(I32).rearrange("(h q j) c -> h j q c", h=2, q=2)
-            for h in range(2):
-                queue.dma_start(out=tile[64 * h : 64 * h + 4, :].bitcast(I32).rearrange("p (q c) -> p q c", q=2), in_=rows[h])
+        def load_fp4_plane(tile, scales):
+            rows = scales[0].bitcast(I32).rearrange("(u s j) c -> u j s c", u=2, s=2)
+            for u in range(2):
+                nc.sync.dma_start(out=tile[64 * u : 64 * u + 4, :].bitcast(I32).rearrange("p (s c) -> p s c", s=2), in_=rows[u])
 
-        def spread_plane(tile):
+        def spread_fp4_plane(tile):
             words = tile[:].bitcast(I32)
-            for h in range(2):
-                nc.vector.tensor_copy(
-                    out=words[64 * h + 32 : 64 * h + 36, :plane_words], in_=words[64 * h : 64 * h + 4, plane_words:]
-                )
+            block = TOKENS // 4
+            for u in range(2):
+                nc.vector.tensor_copy(out=words[64 * u + 32 : 64 * u + 36, :block], in_=words[64 * u : 64 * u + 4, block:])
 
-        draft_plane = plane_tile(nc.vector, "draft_plane")
-        cache_plane = plane_tile(nc.vector, "cache_plane")
-        arch_plane = plane_tile(nc.vector, "arch_plane")
+        draft_planes = sb.tile([P, DRAFT_PASS], U8, name="draft_planes", align_bytes=64)
+        nc.vector.memset(draft_planes[:].bitcast(I32), 0)
+        cache_plane = fp4_plane("cache_plane")
+        arch_plane = fp4_plane("arch_plane")
         f1 = [sb.tile([P, TOKENS], F32, name="f1_%d" % k) for k in range(2)]
-        nc.vector.memset(f1[0][:], 0.0)
-        nc.vector.memset(f1[1][:], 0.0)
+        for window in f1:
+            nc.vector.memset(window[:], 0.0)
 
         q_raw = sb.tile([P, PACK, P], F32, name="q_raw")
-        nc.sync.dma_start(out=q_raw[:], in_=query.rearrange("(p j) q -> p j q", j=PACK))
-        load_plane(nc.sync, draft_plane, draft_scales)
-        draft_rows = draft_words[0].rearrange("p n t -> p (n t)").bitcast(I32)
+        nc.sync.dma_start(out=q_raw[:], in_=query.rearrange("(p t) q -> p t q", t=PACK))
+        draft_rows = draft_scales[0].bitcast(I32).rearrange("(g j) (n c) -> g n j c", g=4, n=4)
+        for g in range(4):
+            nc.sync.dma_start(out=draft_planes[32 * g : 32 * g + 16, :].bitcast(I32), in_=draft_rows[g])
+        draft_as_words = draft_words[0].rearrange("p n t -> p (n t)").bitcast(I32)
         draft_codes = []
         for n in range(2):
             tile = sb.tile([P, BANK], I32, name="draft_codes%d" % n, align_bytes=64)
-            nc.sync.dma_start(out=tile[:], in_=draft_rows[:, n * BANK : (n + 1) * BANK])
+            nc.sync.dma_start(out=tile[:], in_=draft_as_words[:, n * BANK : (n + 1) * BANK])
             draft_codes.append(tile)
-        load_plane(nc.sync, cache_plane, cache_scales)
+        load_fp4_plane(cache_plane, cache_scales)
         cache_codes = sb.tile([P, 2 * TOKENS], U8, name="cache_codes", align_bytes=64)
         nc.sync.dma_start(out=cache_codes[:].bitcast(I32), in_=cache_words[0].bitcast(I32))
-        load_plane(nc.sync, arch_plane, arch_scales)
+        load_fp4_plane(arch_plane, arch_scales)
         lists = {}
 
-        def load_list(name, src):
-            lists[name] = sb.tile([P, SLOTS // 16], U16, name="list_" + name)
-            nc.sync.dma_start(lists[name][:], src)
+        def load_list(name, source):
+            lists[name] = sb.tile([P, SLOTS // PER_COLUMN], U16, name="list_" + name)
+            nc.sync.dma_start(lists[name][:], source)
 
-        load_list("draft", offs2)
-        arch_codes = sb.tile([P, 2 * TOKENS], U8, name="arch_codes", tag="arch_then_gb1", align_bytes=64)
+        def entries(name, slots):
+            return lists[name][:, slots.start // PER_COLUMN : slots.stop // PER_COLUMN]
+
+        load_list("idx2", offs2)
+        arch_codes = sb.tile([P, 2 * TOKENS], U8, name="arch_codes", tag="arch_codes_then_gb1", align_bytes=64)
         nc.sync.dma_start(out=arch_codes[:].bitcast(I32), in_=arch_words[0].bitcast(I32))
-        load_list("arch", offs3)
-        load_list("cache", offs)
-        load_list("put", offs4)
-
-        def half_list(name, h):
-            return lists[name][:, h * LIST_COLS : (h + 1) * LIST_COLS]
+        load_list("idx3", offs3)
+        load_list("idx", offs)
+        load_list("idx4", offs4)
 
         q_bf = sb.tile([P, P, PACK], BF16, name="q_bf", align_bytes=64)
-        nc.vector.tensor_copy(out=q_bf[:], in_=q_raw[:].rearrange("p j q -> p q j"))
-        spread_plane(draft_plane)
+        nc.vector.tensor_copy(out=q_bf[:], in_=q_raw[:].rearrange("p t q -> p q t"))
         q_codes = sb.tile([P, P], U32, name="q_codes", align_bytes=64)
         q_plane = sb.tile([P, P], U8, name="q_plane", align_bytes=64)
-        nc.vector.quantize_mx(out=q_codes[:].bitcast(FP8X4), scales=q_plane[:], in_=q_bf[:].rearrange("p q j -> p (q j)"))
-        spread_plane(cache_plane)
-        spread_plane(arch_plane)
+        nc.vector.quantize_mx(out=q_codes[:].bitcast(FP8X4), scales=q_plane[:], in_=q_bf[:].rearrange("p q t -> p (q t)"))
+        spread_fp4_plane(cache_plane)
+        spread_fp4_plane(arch_plane)
 
-        def score(name, n, rhs, rhs_scale):
-            bank = ps.tile([P, BANK], F32, name="bank_%s%d" % (name, n))
+        def score(scores, keys, keys_plane):
             nc.tensor.matmul_mx(
-                out=bank[:], lhsT=q_codes[:].bitcast(FP8X4), lhsT_scale=q_plane[:], rhs=rhs, rhs_scale=rhs_scale, start=True, stop=True
+                out=scores, lhsT=q_codes[:].bitcast(FP8X4), lhsT_scale=q_plane[:], rhs=keys, rhs_scale=keys_plane, start=True, stop=True
             )
-            return bank
 
-        b_banks = [score("b", n, draft_codes[n][:].bitcast(FP8X4), draft_plane[:, n * BANK : (n + 1) * BANK]) for n in range(2)]
-        a_banks = [
-            score("a", n, cache_codes[:, 2 * n * BANK : 2 * (n + 1) * BANK].bitcast(FP4X4), cache_plane[:, n * BANK : (n + 1) * BANK])
-            for n in range(2)
-        ]
-        c_banks = [
-            score(
-                "c",
-                n,
-                arch_codes[:, 2 * n * BANK : 2 * (n + 1) * BANK].bitcast(FP4X4),
-                arch_plane[:, n * BANK : (n + 1) * BANK],
-            )
-            for n in range(2)
-        ]
+        def fp4_scores(name, codes, plane):
+            banks = []
+            for n in range(2):
+                bank = ps.tile([P, BANK], F32, name="bank_%s%d" % (name, n))
+                score(bank[:], codes[:, 2 * n * BANK : 2 * (n + 1) * BANK].bitcast(FP4X4), plane[:, n * BANK : (n + 1) * BANK])
+                banks.append(bank)
+            return banks
 
+        b_banks = []
+        for n in range(2):
+            bank = ps.tile([P, BANK], F32, name="bank_b%d" % n)
+            for m in range(2):
+                cols = slice(m * DRAFT_PASS, (m + 1) * DRAFT_PASS)
+                score(bank[:, cols], draft_codes[n][:, cols].bitcast(FP8X4), draft_planes[4 * (2 * n + m) : P, :])
+            b_banks.append(bank)
+        a_banks = fp4_scores("a", cache_codes, cache_plane)
+        c_banks = fp4_scores("c", arch_codes, arch_plane)
+
+        halves = (slice(0, HALF), slice(HALF, SLOTS))
         a = sb.tile([P, TOKENS], F32, name="a")
         b = sb.tile([P, TOKENS], F32, name="b")
         c0 = sb.tile([P, TOKENS], F32, name="c0")
@@ -127,54 +129,54 @@ def tile_attend_gapenergies_three_kernel(
         dv0 = sb.tile([P, HALF], F32, name="dv0")
         w0 = sb.tile([P, HALF], F32, name="w0")
         gc1 = sb.tile([P, HALF], F32, name="gc1")
-        d1 = sb.tile([P, SLOTS], F32, name="d1")
-        wide = sb.tile([P, HALF + TOKENS], F32, name="wide")
-        wv1 = wide[:, :SLOTS]
-        pieces = (slice(0, FIRST), slice(FIRST, HALF))
-        r0 = [sb.tile([P, piece.stop - piece.start], F32, name="r0_%d" % k) for k, piece in enumerate(pieces)]
+        dwv1 = sb.tile([P, 2 * HALF], F32, name="dwv1")
+        shared = sb.tile([P, HALF + TOKENS], F32, name="shared")
+        wv1 = shared[:, : 2 * HALF]
+        partial_cc = shared[:, HALF:]
+        pieces0 = (slice(0, FIRST), slice(FIRST, HALF))
+        r0 = [sb.tile([P, piece.stop - piece.start], F32, name="r0_%d" % k) for k, piece in enumerate(pieces0)]
         v0_rest = sb.tile([P, HALF - FIRST], F32, name="v0_rest")
-        v0 = [wv1[:, HALF : HALF + FIRST], v0_rest[:]]
+        v0 = [shared[:, HALF : HALF + FIRST], v0_rest[:]]
         r1 = sb.tile([P, HALF], F32, name="r1")
-        w = [w0[:], wv1[:, :HALF]]
 
         for whole, banks in ((b, b_banks), (a, a_banks)):
             for n in range(2):
                 nc.scalar.copy(whole[:, n * BANK : (n + 1) * BANK], banks[n][:])
-        nc.vector.tensor_copy(gb0[:], b[:].indirect(half_list("draft", 0)))
+        nc.vector.tensor_copy(gb0[:], b[:].indirect(entries("idx2", halves[0])))
         nc.vector.tensor_copy(c0[:, :BANK], c_banks[0][:])
         nc.scalar.copy(c0[:, BANK:], c_banks[1][:])
-        nc.vector.tensor_tensor(dw0[:], a[:].indirect(half_list("cache", 0)), gb0[:], ALU.subtract)
-        nc.vector.tensor_tensor(dv0[:], c0[:].indirect(half_list("arch", 0)), gb0[:], ALU.subtract)
-        gb1 = sb.tile([P, HALF], F32, name="gb1", tag="arch_then_gb1", align_bytes=64)
-        nc.scalar.activation(gb1[:], b[:].indirect(half_list("draft", 1)), ACT.Copy)
-        nc.scalar.activation(gc1[:], c0[:].indirect(half_list("arch", 1)), ACT.Copy)
+        nc.vector.tensor_tensor(dw0[:], a[:].indirect(entries("idx", halves[0])), gb0[:], ALU.subtract)
+        nc.vector.tensor_tensor(dv0[:], c0[:].indirect(entries("idx3", halves[0])), gb0[:], ALU.subtract)
+        gb1 = sb.tile([P, HALF], F32, name="gb1", tag="arch_codes_then_gb1", align_bytes=64)
+        nc.scalar.activation(gb1[:], b[:].indirect(entries("idx2", halves[1])), ACT.Copy)
+        nc.scalar.activation(gc1[:], c0[:].indirect(entries("idx3", halves[1])), ACT.Copy)
         nc.scalar.activation(w0[:], dw0[:], ACT.Abs)
-        for k, piece in enumerate(pieces):
+        for k, piece in enumerate(pieces0):
             nc.scalar.activation(v0[k], dv0[:, piece], ACT.Abs)
-        nc.vector.tensor_tensor(d1[:, :HALF], a[:].indirect(half_list("cache", 1)), gb1[:], ALU.subtract)
-        nc.vector.tensor_tensor(d1[:, HALF:], gc1[:], gb1[:], ALU.subtract)
-        for k, piece in enumerate(pieces):
+        nc.vector.tensor_tensor(dwv1[:, :HALF], a[:].indirect(entries("idx", halves[1])), gb1[:], ALU.subtract)
+        nc.vector.tensor_tensor(dwv1[:, HALF:], gc1[:], gb1[:], ALU.subtract)
+        for k, piece in enumerate(pieces0):
             nc.vector.tensor_tensor(r0[k][:], w0[:, piece], v0[k], ALU.subtract)
-            nc.scalar.activation(f1[k][:].indirect(lists["put"][:, piece.start // 16 : piece.stop // 16]), r0[k][:], ACT.Copy)
-        nc.vector.scalar_tensor_tensor(wv1, d1[:], -1.0, d1[:], ALU.mult, ALU.max)
+            nc.scalar.activation(f1[k][:].indirect(entries("idx4", piece)), r0[k][:], ACT.Copy)
+        nc.vector.scalar_tensor_tensor(wv1, dwv1[:], -1.0, dwv1[:], ALU.mult, ALU.max)
         nc.vector.tensor_tensor(r1[:], wv1[:, :HALF], wv1[:, HALF:], ALU.subtract)
-        nc.scalar.activation(f1[0][:].indirect(half_list("put", 1)), r1[:], ACT.Copy)
+        nc.scalar.activation(f1[0][:].indirect(entries("idx4", halves[1])), r1[:], ACT.Copy)
 
         cc = sb.tile([P, TOKENS], F32, name="cc")
-        part = wide[:, HALF:]
-        nc.vector.tensor_tensor(part, c0[:], f1[1][:], ALU.add)
-        nc.vector.tensor_tensor(cc[:], part, f1[0][:], ALU.add)
+        nc.vector.tensor_tensor(partial_cc, c0[:], f1[1][:], ALU.add)
+        nc.vector.tensor_tensor(cc[:], partial_cc, f1[0][:], ALU.add)
+
         dy0 = sb.tile([P, HALF], F32, name="dy0")
         y0 = sb.tile([P, HALF], F32, name="y0")
-        gcc = sb.tile([P, HALF], F32, name="gcc")
-        nc.vector.tensor_tensor(dy0[:], cc[:].indirect(half_list("arch", 0)), w[0], ALU.subtract)
-        nc.scalar.activation(gcc[:], cc[:].indirect(half_list("arch", 1)), ACT.Copy)
+        gcc1 = sb.tile([P, HALF], F32, name="gcc1")
+        nc.vector.tensor_tensor(dy0[:], cc[:].indirect(entries("idx3", halves[0])), w0[:], ALU.subtract)
+        nc.scalar.activation(gcc1[:], cc[:].indirect(entries("idx3", halves[1])), ACT.Copy)
         nc.scalar.activation(y0[:], dy0[:], ACT.Abs)
-        nc.sync.dma_start(out=out[:, :HALF], in_=y0[:])
-        for k in range(2):
-            cols = slice(k * QUARTER, (k + 1) * QUARTER)
-            dy1 = sb.tile([P, QUARTER], F32, name="dy1_%d" % k)
-            y1 = sb.tile([P, QUARTER], F32, name="y1_%d" % k)
-            nc.vector.tensor_tensor(dy1[:], gcc[:, cols], wv1[:, cols], ALU.subtract)
+        nc.sync.dma_start(out=out[:, halves[0]], in_=y0[:])
+        for k in range(HALF // STORE):
+            cols = slice(k * STORE, (k + 1) * STORE)
+            dy1 = sb.tile([P, STORE], F32, name="dy1_%d" % k)
+            y1 = sb.tile([P, STORE], F32, name="y1_%d" % k)
+            nc.vector.tensor_tensor(dy1[:], gcc1[:, cols], wv1[:, cols], ALU.subtract)
             nc.scalar.activation(y1[:], dy1[:], ACT.Abs)
             nc.sync.dma_start(out=out[:, HALF + cols.start : HALF + cols.stop], in_=y1[:])

from contextlib import ExitStack

import concourse.mybir as mybir

F32 = mybir.dt.float32
BF16 = mybir.dt.bfloat16
I32 = mybir.dt.int32
U32 = mybir.dt.uint32
U16 = mybir.dt.uint16
U8 = mybir.dt.uint8
FP8X4 = mybir.dt.float8_e4m3fn_x4
FP4X4 = mybir.dt.float4_e2m1fn_x4
ALU = mybir.AluOpType
ACT = mybir.ActivationFunctionType

P = 128
PACK = 4
TOKENS = 1024
SLOTS = 512
BANK = 512
PER_COLUMN = 16
HALF = SLOTS // 2
STORE = SLOTS // 4
DRAFT_PASS = TOKENS // 4
FIRST = 64
FLOPS = 3 * 2 * 512 * P * TOKENS


def tile_attend_gapenergies_three_kernel(
    tc, query, cache_words, cache_scales, draft_words, draft_scales, arch_words, arch_scales, offs, offs2, offs3, offs4, out
):
    nc = tc.nc
    with ExitStack() as ctx:
        sb = ctx.enter_context(tc.tile_pool(name="sb", bufs=1))
        ps = ctx.enter_context(tc.psum_pool(name="ps", bufs=1))

        def fp4_plane(name):
            tile = sb.tile([P, 2 * TOKENS], U8, name=name, align_bytes=64)
            nc.vector.memset(tile[:, :TOKENS].bitcast(I32), 0)
            return tile

        def load_fp4_plane(tile, scales):
            rows = scales[0].bitcast(I32).rearrange("(u s j) c -> u j s c", u=2, s=2)
            for u in range(2):
                nc.sync.dma_start(out=tile[64 * u : 64 * u + 4, :].bitcast(I32).rearrange("p (s c) -> p s c", s=2), in_=rows[u])

        def spread_fp4_plane(tile):
            words = tile[:].bitcast(I32)
            block = TOKENS // 4
            for u in range(2):
                nc.vector.tensor_copy(out=words[64 * u + 32 : 64 * u + 36, :block], in_=words[64 * u : 64 * u + 4, block:])

        draft_planes = sb.tile([P, DRAFT_PASS], U8, name="draft_planes", align_bytes=64)
        nc.vector.memset(draft_planes[:].bitcast(I32), 0)
        cache_plane = fp4_plane("cache_plane")
        arch_plane = fp4_plane("arch_plane")
        f1 = [sb.tile([P, TOKENS], F32, name="f1_%d" % k) for k in range(2)]
        for window in f1:
            nc.vector.memset(window[:], 0.0)

        q_raw = sb.tile([P, PACK, P], F32, name="q_raw")
        nc.sync.dma_start(out=q_raw[:], in_=query.rearrange("(p t) q -> p t q", t=PACK))
        draft_rows = draft_scales[0].bitcast(I32).rearrange("(g j) (n c) -> g n j c", g=4, n=4)
        for g in range(4):
            nc.sync.dma_start(out=draft_planes[32 * g : 32 * g + 16, :].bitcast(I32), in_=draft_rows[g])
        draft_as_words = draft_words[0].rearrange("p n t -> p (n t)").bitcast(I32)
        draft_codes = []
        for n in range(2):
            tile = sb.tile([P, BANK], I32, name="draft_codes%d" % n, align_bytes=64)
            nc.sync.dma_start(out=tile[:], in_=draft_as_words[:, n * BANK : (n + 1) * BANK])
            draft_codes.append(tile)
        load_fp4_plane(cache_plane, cache_scales)
        cache_codes = sb.tile([P, 2 * TOKENS], U8, name="cache_codes", align_bytes=64)
        nc.sync.dma_start(out=cache_codes[:].bitcast(I32), in_=cache_words[0].bitcast(I32))
        load_fp4_plane(arch_plane, arch_scales)
        lists = {}

        def load_list(name, source):
            lists[name] = sb.tile([P, SLOTS // PER_COLUMN], U16, name="list_" + name)
            nc.sync.dma_start(lists[name][:], source)

        def entries(name, slots):
            return lists[name][:, slots.start // PER_COLUMN : slots.stop // PER_COLUMN]

        load_list("idx2", offs2)
        arch_codes = sb.tile([P, 2 * TOKENS], U8, name="arch_codes", tag="arch_codes_then_gb1", align_bytes=64)
        nc.sync.dma_start(out=arch_codes[:].bitcast(I32), in_=arch_words[0].bitcast(I32))
        load_list("idx3", offs3)
        load_list("idx", offs)
        load_list("idx4", offs4)

        q_bf = sb.tile([P, P, PACK], BF16, name="q_bf", align_bytes=64)
        nc.vector.tensor_copy(out=q_bf[:], in_=q_raw[:].rearrange("p t q -> p q t"))
        q_codes = sb.tile([P, P], U32, name="q_codes", align_bytes=64)
        q_plane = sb.tile([P, P], U8, name="q_plane", align_bytes=64)
        nc.vector.quantize_mx(out=q_codes[:].bitcast(FP8X4), scales=q_plane[:], in_=q_bf[:].rearrange("p q t -> p (q t)"))
        spread_fp4_plane(cache_plane)
        spread_fp4_plane(arch_plane)

        def score(scores, keys, keys_plane):
            nc.tensor.matmul_mx(
                out=scores, lhsT=q_codes[:].bitcast(FP8X4), lhsT_scale=q_plane[:], rhs=keys, rhs_scale=keys_plane, start=True, stop=True
            )

        def fp4_scores(name, codes, plane):
            banks = []
            for n in range(2):
                bank = ps.tile([P, BANK], F32, name="bank_%s%d" % (name, n))
                score(bank[:], codes[:, 2 * n * BANK : 2 * (n + 1) * BANK].bitcast(FP4X4), plane[:, n * BANK : (n + 1) * BANK])
                banks.append(bank)
            return banks

        b_banks = []
        for n in range(2):
            bank = ps.tile([P, BANK], F32, name="bank_b%d" % n)
            for m in range(2):
                cols = slice(m * DRAFT_PASS, (m + 1) * DRAFT_PASS)
                score(bank[:, cols], draft_codes[n][:, cols].bitcast(FP8X4), draft_planes[4 * (2 * n + m) : P, :])
            b_banks.append(bank)
        a_banks = fp4_scores("a", cache_codes, cache_plane)
        c_banks = fp4_scores("c", arch_codes, arch_plane)

        halves = (slice(0, HALF), slice(HALF, SLOTS))
        a = sb.tile([P, TOKENS], F32, name="a")
        b = sb.tile([P, TOKENS], F32, name="b")
        c0 = sb.tile([P, TOKENS], F32, name="c0")
        gb0 = sb.tile([P, HALF], F32, name="gb0")
        dw0 = sb.tile([P, HALF], F32, name="dw0")
        dv0 = sb.tile([P, HALF], F32, name="dv0")
        w0 = sb.tile([P, HALF], F32, name="w0")
        gc1 = sb.tile([P, HALF], F32, name="gc1")
        dwv1 = sb.tile([P, 2 * HALF], F32, name="dwv1")
        shared = sb.tile([P, HALF + TOKENS], F32, name="shared")
        wv1 = shared[:, : 2 * HALF]
        partial_cc = shared[:, HALF:]
        pieces0 = (slice(0, FIRST), slice(FIRST, HALF))
        r0 = [sb.tile([P, piece.stop - piece.start], F32, name="r0_%d" % k) for k, piece in enumerate(pieces0)]
        v0_rest = sb.tile([P, HALF - FIRST], F32, name="v0_rest")
        v0 = [shared[:, HALF : HALF + FIRST], v0_rest[:]]
        r1 = sb.tile([P, HALF], F32, name="r1")

        for whole, banks in ((b, b_banks), (a, a_banks)):
            for n in range(2):
                nc.scalar.copy(whole[:, n * BANK : (n + 1) * BANK], banks[n][:])
        nc.vector.tensor_copy(gb0[:], b[:].indirect(entries("idx2", halves[0])))
        nc.vector.tensor_copy(c0[:, :BANK], c_banks[0][:])
        nc.scalar.copy(c0[:, BANK:], c_banks[1][:])
        nc.vector.tensor_tensor(dw0[:], a[:].indirect(entries("idx", halves[0])), gb0[:], ALU.subtract)
        nc.vector.tensor_tensor(dv0[:], c0[:].indirect(entries("idx3", halves[0])), gb0[:], ALU.subtract)
        gb1 = sb.tile([P, HALF], F32, name="gb1", tag="arch_codes_then_gb1", align_bytes=64)
        nc.scalar.activation(gb1[:], b[:].indirect(entries("idx2", halves[1])), ACT.Copy)
        nc.scalar.activation(gc1[:], c0[:].indirect(entries("idx3", halves[1])), ACT.Copy)
        nc.scalar.activation(w0[:], dw0[:], ACT.Abs)
        for k, piece in enumerate(pieces0):
            nc.scalar.activation(v0[k], dv0[:, piece], ACT.Abs)
        nc.vector.tensor_tensor(dwv1[:, :HALF], a[:].indirect(entries("idx", halves[1])), gb1[:], ALU.subtract)
        nc.vector.tensor_tensor(dwv1[:, HALF:], gc1[:], gb1[:], ALU.subtract)
        for k, piece in enumerate(pieces0):
            nc.vector.tensor_tensor(r0[k][:], w0[:, piece], v0[k], ALU.subtract)
            nc.scalar.activation(f1[k][:].indirect(entries("idx4", piece)), r0[k][:], ACT.Copy)
        nc.vector.scalar_tensor_tensor(wv1, dwv1[:], -1.0, dwv1[:], ALU.mult, ALU.max)
        nc.vector.tensor_tensor(r1[:], wv1[:, :HALF], wv1[:, HALF:], ALU.subtract)
        nc.scalar.activation(f1[0][:].indirect(entries("idx4", halves[1])), r1[:], ACT.Copy)

        cc = sb.tile([P, TOKENS], F32, name="cc")
        nc.vector.tensor_tensor(partial_cc, c0[:], f1[1][:], ALU.add)
        nc.vector.tensor_tensor(cc[:], partial_cc, f1[0][:], ALU.add)

        dy0 = sb.tile([P, HALF], F32, name="dy0")
        y0 = sb.tile([P, HALF], F32, name="y0")
        gcc1 = sb.tile([P, HALF], F32, name="gcc1")
        nc.vector.tensor_tensor(dy0[:], cc[:].indirect(entries("idx3", halves[0])), w0[:], ALU.subtract)
        nc.scalar.activation(gcc1[:], cc[:].indirect(entries("idx3", halves[1])), ACT.Copy)
        nc.scalar.activation(y0[:], dy0[:], ACT.Abs)
        nc.sync.dma_start(out=out[:, halves[0]], in_=y0[:])
        for k in range(HALF // STORE):
            cols = slice(k * STORE, (k + 1) * STORE)
            dy1 = sb.tile([P, STORE], F32, name="dy1_%d" % k)
            y1 = sb.tile([P, STORE], F32, name="y1_%d" % k)
            nc.vector.tensor_tensor(dy1[:], gcc1[:, cols], wv1[:, cols], ALU.subtract)
            nc.scalar.activation(y1[:], dy1[:], ACT.Abs)
            nc.sync.dma_start(out=out[:, HALF + cols.start : HALF + cols.stop], in_=y1[:])
